import numpy as np
import ml_dtypes

BF16 = ml_dtypes.bfloat16


def bf(x):
    return np.asarray(x, np.float32).astype(BF16)


def f32(x):
    return np.asarray(x, np.float32)


def f64(x):
    return np.asarray(x).astype(np.float64)


def striped(idx):
    return np.tile(idx.reshape(-1, 16).T, (8, 1))


def rows(idx, k):
    return np.tile(idx, (k, 1))


def look(tab, idx):
    return np.take_along_axis(f64(tab), rows(idx, len(tab)), axis=1)


K, S, V, N = 512, 2048, 1024, 1024


def silu(v):
    return v / (1.0 + np.exp(-v))


def setup_inputs():
    return {"tab": f32(np.random.standard_normal((2, K, S))), "offs": striped(np.random.permutation(S)[:N])}


def reference(tab, offs):
    idx = offs[:16].T.reshape(-1)
    x = silu(look(tab[0], idx)) * look(tab[1], idx)
    return x

@@ -1,0 +1,46 @@
+import concourse.mybir as mybir
+
+F32 = mybir.dt.float32
+U16 = mybir.dt.uint16
+SILU = mybir.ActivationFunctionType.Silu
+MULT = mybir.AluOpType.mult
+
+P = 128
+ENTRIES_PER_COLUMN = 16
+PIECE = 512
+
+
+def tile_lookup_glu_silu_out_kernel(tc, tab, offs, out):
+    nc = tc.nc
+    tables, rows, places = tab.shape
+    list_columns = offs.shape[1]
+    entries = ENTRIES_PER_COLUMN * list_columns
+    blocks = rows // P
+    piece_columns = PIECE // ENTRIES_PER_COLUMN
+
+    with tc.tile_pool(name="held", bufs=1) as held:
+        offsets = held.tile([P, list_columns], U16, name="offsets")
+        nc.sync.dma_start(offsets[:], offs)
+
+        gate_windows = []
+        value_windows = []
+        for b in range(blocks):
+            block_rows = slice(b * P, (b + 1) * P)
+            gate_window = held.tile([P, places], F32, name=f"gate_window{b}")
+            nc.sync.dma_start(gate_window[:], tab[0, block_rows, :])
+            gate_windows.append(gate_window)
+            value_window = held.tile([P, places], F32, name=f"value_window{b}")
+            nc.sync.dma_start(value_window[:], tab[1, block_rows, :])
+            value_windows.append(value_window)
+
+        for b in range(blocks):
+            block_rows = slice(b * P, (b + 1) * P)
+            gate = held.tile([P, entries], F32, name=f"gate{b}")
+            x = held.tile([P, entries], F32, name=f"x{b}")
+            for first in range(0, entries, PIECE):
+                piece = slice(first, first + PIECE)
+                first_column = first // ENTRIES_PER_COLUMN
+                list_piece = offsets[:, first_column : first_column + piece_columns]
+                nc.scalar.activation(gate[:, piece], gate_windows[b][:].indirect(list_piece), SILU)
+                nc.vector.tensor_tensor(x[:, piece], value_windows[b][:].indirect(list_piece), gate[:, piece], MULT)
+            nc.sync.dma_start(out[block_rows, :], x[:])

@@ -19,9 +19,6 @@ def tile_lookup_glu_silu_out_kernel(tc, tab, offs, out):
     piece_columns = PIECE // ENTRIES_PER_COLUMN
 
     with tc.tile_pool(name="held", bufs=1) as held:
-        offsets = held.tile([P, list_columns], U16, name="offsets")
-        nc.sync.dma_start(offsets[:], offs)
-
         gate_windows = []
         value_windows = []
         for b in range(blocks):
@@ -29,6 +26,9 @@ def tile_lookup_glu_silu_out_kernel(tc, tab, offs, out):
             gate_window = held.tile([P, places], F32, name=f"gate_window{b}")
             nc.sync.dma_start(gate_window[:], tab[0, block_rows, :])
             gate_windows.append(gate_window)
+            if b == 0:
+                offsets = held.tile([P, list_columns], U16, name="offsets")
+                nc.sync.dma_start(offsets[:], offs)
             value_window = held.tile([P, places], F32, name=f"value_window{b}")
             nc.sync.dma_start(value_window[:], tab[1, block_rows, :])
             value_windows.append(value_window)
@@ -43,4 +43,4 @@ def tile_lookup_glu_silu_out_kernel(tc, tab, offs, out):
                 list_piece = offsets[:, first_column : first_column + piece_columns]
                 nc.scalar.activation(gate[:, piece], gate_windows[b][:].indirect(list_piece), SILU)
                 nc.vector.tensor_tensor(x[:, piece], value_windows[b][:].indirect(list_piece), gate[:, piece], MULT)
-            nc.sync.dma_start(out[block_rows, :], x[:])
+                nc.sync.dma_start(out[block_rows, piece], x[:, piece])

@@ -7,16 +7,23 @@ MULT = mybir.AluOpType.mult
 
 P = 128
 ENTRIES_PER_COLUMN = 16
-PIECE = 512
+SILU_PIECE = 512
+LAST_PRODUCT_PIECE = 256
+
+
+def pieces(offsets, entries, length):
+    return [
+        (slice(first, first + length), offsets[:, first // ENTRIES_PER_COLUMN : (first + length) // ENTRIES_PER_COLUMN])
+        for first in range(0, entries, length)
+    ]
 
 
 def tile_lookup_glu_silu_out_kernel(tc, tab, offs, out):
     nc = tc.nc
-    tables, rows, places = tab.shape
+    rows, places = tab.shape[1:]
     list_columns = offs.shape[1]
     entries = ENTRIES_PER_COLUMN * list_columns
     blocks = rows // P
-    piece_columns = PIECE // ENTRIES_PER_COLUMN
 
     with tc.tile_pool(name="held", bufs=1) as held:
         gate_windows = []
@@ -37,10 +44,9 @@ def tile_lookup_glu_silu_out_kernel(tc, tab, offs, out):
             block_rows = slice(b * P, (b + 1) * P)
             gate = held.tile([P, entries], F32, name=f"gate{b}")
             x = held.tile([P, entries], F32, name=f"x{b}")
-            for first in range(0, entries, PIECE):
-                piece = slice(first, first + PIECE)
-                first_column = first // ENTRIES_PER_COLUMN
-                list_piece = offsets[:, first_column : first_column + piece_columns]
+            for piece, list_piece in pieces(offsets, entries, SILU_PIECE):
                 nc.scalar.activation(gate[:, piece], gate_windows[b][:].indirect(list_piece), SILU)
+            product_piece = LAST_PRODUCT_PIECE if b == blocks - 1 else entries
+            for piece, list_piece in pieces(offsets, entries, product_piece):
                 nc.vector.tensor_tensor(x[:, piece], value_windows[b][:].indirect(list_piece), gate[:, piece], MULT)
                 nc.sync.dma_start(out[block_rows, piece], x[:, piece])

import concourse.mybir as mybir

F32 = mybir.dt.float32
U16 = mybir.dt.uint16
SILU = mybir.ActivationFunctionType.Silu
MULT = mybir.AluOpType.mult

P = 128
ENTRIES_PER_COLUMN = 16
SILU_PIECE = 512
LAST_PRODUCT_PIECE = 256


def pieces(offsets, entries, length):
    return [
        (slice(first, first + length), offsets[:, first // ENTRIES_PER_COLUMN : (first + length) // ENTRIES_PER_COLUMN])
        for first in range(0, entries, length)
    ]


def tile_lookup_glu_silu_out_kernel(tc, tab, offs, out):
    nc = tc.nc
    rows, places = tab.shape[1:]
    list_columns = offs.shape[1]
    entries = ENTRIES_PER_COLUMN * list_columns
    blocks = rows // P

    with tc.tile_pool(name="held", bufs=1) as held:
        gate_windows = []
        value_windows = []
        for b in range(blocks):
            block_rows = slice(b * P, (b + 1) * P)
            gate_window = held.tile([P, places], F32, name=f"gate_window{b}")
            nc.sync.dma_start(gate_window[:], tab[0, block_rows, :])
            gate_windows.append(gate_window)
            if b == 0:
                offsets = held.tile([P, list_columns], U16, name="offsets")
                nc.sync.dma_start(offsets[:], offs)
            value_window = held.tile([P, places], F32, name=f"value_window{b}")
            nc.sync.dma_start(value_window[:], tab[1, block_rows, :])
            value_windows.append(value_window)

        for b in range(blocks):
            block_rows = slice(b * P, (b + 1) * P)
            gate = held.tile([P, entries], F32, name=f"gate{b}")
            x = held.tile([P, entries], F32, name=f"x{b}")
            for piece, list_piece in pieces(offsets, entries, SILU_PIECE):
                nc.scalar.activation(gate[:, piece], gate_windows[b][:].indirect(list_piece), SILU)
            product_piece = LAST_PRODUCT_PIECE if b == blocks - 1 else entries
            for piece, list_piece in pieces(offsets, entries, product_piece):
                nc.vector.tensor_tensor(x[:, piece], value_windows[b][:].indirect(list_piece), gate[:, piece], MULT)
                nc.sync.dma_start(out[block_rows, piece], x[:, piece])
